import numpy as np, ml_dtypes
CORES = [122,123,126,250,251,254,378,379,382,506,507,510]
N = 12
DEG, TK = 3, 512
MASK = [[11,0,1],[0,1,2],[1,2,3],[2,3,4],[3,4,5],[4,5,6],[5,6,7],[6,7,8],[7,8,9],[8,9,10],[9,10,11],[10,11,0]]
def setup_inputs(rng):
    return {"x": rng.standard_normal((N, 128, TK), dtype=np.float32).astype(ml_dtypes.bfloat16), "w": rng.standard_normal((N, 128, DEG * 128), dtype=np.float32).astype(ml_dtypes.bfloat16)}
def setup_inputs_big(rng):
    d = setup_inputs(rng)
    for k in ("x", "w"): d[k] = (d[k].astype(np.float32) * 1024.0).astype(d[k].dtype)
    return d
def setup_inputs_small(rng):
    d = setup_inputs(rng)
    for k in ("x", "w"): d[k] = (d[k].astype(np.float32) * (1 / 1024.0)).astype(d[k].dtype)
    return d
def setup_inputs_apart(rng):
    d = setup_inputs(rng)
    f = (10.0 ** rng.permutation(np.linspace(-1.5, 1.5, N))).astype(np.float32).reshape(N, 1, 1)
    for k in ("x", "w"): d[k] = (d[k].astype(np.float32) * f).astype(d[k].dtype)
    return d
def reference(x, w):
    X, W = x.astype(np.float64), w.astype(np.float64)
    y = np.zeros((N, 128, TK))
    for r in range(N):
        for i, j in enumerate(MASK[r]):
            y[r] += W[r][:, 128 * i:128 * i + 128].T @ X[j]
    return {"y": y.astype(ml_dtypes.bfloat16 if x.dtype != np.float64 else np.float64)}

@@ -1,0 +1,106 @@
+from concourse.bass import DstId, RemoteDMATransfer
+
+P, TK, DEG = 128, 512, 3
+NLAND = DEG - 1
+NH = 2
+HW = TK // NH
+ENG = 8
+
+SCRATCH = {
+    "xs": ("sbuf", [P, TK], "bfloat16"),
+    "ws": ("sbuf", [P, DEG * P], "bfloat16"),
+    "ys": ("sbuf", [P, TK], "bfloat16"),
+}
+for _k in range(NLAND):
+    SCRATCH["land%d" % _k] = ("sbuf", [P, TK], "bfloat16")
+for _h in range(NH):
+    SCRATCH["acc%d" % _h] = ("psum", [P, 512], "float32")
+
+SEMAPHORES = (["sx", "sw", "sent"] + ["arr%d" % k for k in range(NLAND)]
+              + ["mm%d" % h for h in range(NH)] + ["cp%d" % h for h in range(NH)] + ["st%d" % h for h in range(NH)])
+
+
+def _bits(m):
+    return [b for b in range(m.bit_length()) if (m >> b) & 1]
+
+
+def _slots(q, T):
+    row = T.tables["MASK"][q]
+    return [i for i in range(len(row)) if row[i] != q]
+
+
+def _plan(j, T, topo):
+    src = T.cores[j]
+    out = []
+    for q in range(len(T.cores)):
+        for k, i in enumerate(_slots(q, T)):
+            if T.tables["MASK"][q][i] == j:
+                out.append((T.cores[q], k))
+    out.sort(key=lambda e: len(_bits(topo.mask(src, e[0]))))
+    every = 0
+    for d, _ in out:
+        every |= topo.mask(src, d)
+    share = len(_bits(every)) // len(out)
+    taken, res = 0, []
+    for d, k in out:
+        block = [b for b in _bits(topo.mask(src, d)) if not (taken >> b) & 1][:share]
+        for b in block:
+            taken |= 1 << b
+        n = min(ENG, len(block))
+        res.append((d, k, sum(1 << b for b in block[::len(block) // n][:n])))
+    return res
+
+
+def rank_program(g, core, T, topo):
+    rank = T.rank_of(core)
+    if rank is None:
+        return
+    row = T.tables["MASK"][rank]
+    sem = T.sem
+
+    g.sync.dma_start(T.xs[:], T.x[:]).then_inc(sem.sx, 16)
+    g.sync.dma_start(T.ws[:], T.w[:]).then_inc(sem.sw, 16)
+
+    plan = _plan(rank, T, topo)
+    g.wait_ge(sem.sx, 16)
+    transfers = []
+    for d, k, m in plan:
+        rid, pid = topo.addr(d, core)
+        transfers.append(RemoteDMATransfer(dst_ids=[DstId(rid=rid, pnc=pid)], dma_engine_mask=m,
+                                           remote_sem=sem["arr%d" % k], src=T.xs[:], dst=T["land%d" % k][:]))
+    g.remote_dma_fused(transfers, local_sem=sem.sent)
+
+    def far(i):
+        s = T.cores[row[i]]
+        return ((topo.host(s), topo.chip(s)) != (topo.host(core), topo.chip(core)), topo.die(s) != topo.die(core))
+
+    slots = _slots(rank, T)
+    own = [i for i in range(len(row)) if row[i] == rank]
+    order = own + sorted(slots, key=far)
+    g.tensor.wait_ge(sem.sx, 16)
+    g.tensor.wait_ge(sem.sw, 16)
+    for n, i in enumerate(order):
+        if i in slots:
+            k = slots.index(i)
+            cnt = [len(_bits(m)) for d, kk, m in _plan(row[i], T, topo) if d == core and kk == k][0]
+            g.tensor.wait_ge(sem["arr%d" % k], cnt)
+            src = T["land%d" % k]
+        else:
+            src = T.xs
+        last = n == len(order) - 1
+        for h in range(NH):
+            mm = g.tensor.matmul(T["acc%d" % h][:, 0:HW], T.ws[:, P * i:P * i + P], src[:, HW * h:HW * h + HW],
+                                 start=(n == 0), stop=last)
+            if last:
+                mm.then_inc(sem["mm%d" % h], 1)
+
+    queues = [g.sync, g.scalar]
+    for h in range(NH):
+        g.vector.wait_ge(sem["mm%d" % h], 1)
+        g.vector.tensor_copy(T.ys[:, HW * h:HW * h + HW], T["acc%d" % h][:, 0:HW]).then_inc(sem["cp%d" % h], 1)
+        q = queues[h % 2]
+        q.wait_ge(sem["cp%d" % h], 1)
+        q.dma_start(T.y[:, HW * h:HW * h + HW], T.ys[:, HW * h:HW * h + HW]).then_inc(sem["st%d" % h], 16)
+    for h in range(NH):
+        queues[h % 2].wait_ge(sem["st%d" % h], 16)
+    g.wait_ge(sem.sent, sum(len(_bits(m)) for _, _, m in plan))

@@ -2,8 +2,9 @@ from concourse.bass import DstId, RemoteDMATransfer
 
 P, TK, DEG = 128, 512, 3
 NLAND = DEG - 1
-NH = 2
-HW = TK // NH
+WID = [128, 256, 128]
+NB = len(WID)
+LO = [sum(WID[:c]) for c in range(NB)]
 ENG = 8
 
 SCRATCH = {
@@ -13,11 +14,12 @@ SCRATCH = {
 }
 for _k in range(NLAND):
     SCRATCH["land%d" % _k] = ("sbuf", [P, TK], "bfloat16")
-for _h in range(NH):
-    SCRATCH["acc%d" % _h] = ("psum", [P, 512], "float32")
+for _c in range(NB):
+    SCRATCH["acc%d" % _c] = ("psum", [P, 512], "float32")
 
-SEMAPHORES = (["sx", "sw", "sent"] + ["arr%d" % k for k in range(NLAND)]
-              + ["mm%d" % h for h in range(NH)] + ["cp%d" % h for h in range(NH)] + ["st%d" % h for h in range(NH)])
+SEMAPHORES = ["sw", "sent"]
+for _c in range(NB):
+    SEMAPHORES += ["sx%d" % _c, "mm%d" % _c, "cp%d" % _c, "st%d" % _c] + ["arr%d_%d" % (k, _c) for k in range(NLAND)]
 
 
 def _bits(m):
@@ -57,18 +59,25 @@ def rank_program(g, core, T, topo):
         return
     row = T.tables["MASK"][rank]
     sem = T.sem
+    queues = [g.sync, g.scalar]
 
-    g.sync.dma_start(T.xs[:], T.x[:]).then_inc(sem.sx, 16)
-    g.sync.dma_start(T.ws[:], T.w[:]).then_inc(sem.sw, 16)
+    def cols(t, c):
+        return t[:, LO[c]:LO[c] + WID[c]]
+
+    for c in range(NB):
+        queues[c % 2].dma_start(cols(T.xs, c), cols(T.x, c)).then_inc(sem["sx%d" % c], 16)
+    queues[NB % 2].dma_start(T.ws[:], T.w[:]).then_inc(sem.sw, 16)
 
     plan = _plan(rank, T, topo)
-    g.wait_ge(sem.sx, 16)
-    transfers = []
-    for d, k, m in plan:
-        rid, pid = topo.addr(d, core)
-        transfers.append(RemoteDMATransfer(dst_ids=[DstId(rid=rid, pnc=pid)], dma_engine_mask=m,
-                                           remote_sem=sem["arr%d" % k], src=T.xs[:], dst=T["land%d" % k][:]))
-    g.remote_dma_fused(transfers, local_sem=sem.sent)
+    for c in range(NB):
+        g.wait_ge(sem["sx%d" % c], 16)
+        transfers = []
+        for d, k, m in plan:
+            rid, pid = topo.addr(d, core)
+            transfers.append(RemoteDMATransfer(dst_ids=[DstId(rid=rid, pnc=pid)], dma_engine_mask=m,
+                                               remote_sem=sem["arr%d_%d" % (k, c)],
+                                               src=cols(T.xs, c), dst=cols(T["land%d" % k], c)))
+        g.remote_dma_fused(transfers, local_sem=sem.sent)
 
     def far(i):
         s = T.cores[row[i]]
@@ -76,31 +85,31 @@ def rank_program(g, core, T, topo):
 
     slots = _slots(rank, T)
     own = [i for i in range(len(row)) if row[i] == rank]
-    order = own + sorted(slots, key=far)
-    g.tensor.wait_ge(sem.sx, 16)
+    away = sorted(slots, key=far)
+
+    def mm(c, i, src, first, last):
+        ins = g.tensor.matmul(T["acc%d" % c][:, 0:WID[c]], T.ws[:, P * i:P * i + P], cols(src, c), start=first, stop=last)
+        if last:
+            ins.then_inc(sem["mm%d" % c], 1)
+
     g.tensor.wait_ge(sem.sw, 16)
-    for n, i in enumerate(order):
-        if i in slots:
+    for c in range(NB):
+        g.tensor.wait_ge(sem["sx%d" % c], 16)
+        for n, i in enumerate(own):
+            mm(c, i, T.xs, n == 0, False)
+    for c in range(NB):
+        for n, i in enumerate(away):
             k = slots.index(i)
             cnt = [len(_bits(m)) for d, kk, m in _plan(row[i], T, topo) if d == core and kk == k][0]
-            g.tensor.wait_ge(sem["arr%d" % k], cnt)
-            src = T["land%d" % k]
-        else:
-            src = T.xs
-        last = n == len(order) - 1
-        for h in range(NH):
-            mm = g.tensor.matmul(T["acc%d" % h][:, 0:HW], T.ws[:, P * i:P * i + P], src[:, HW * h:HW * h + HW],
-                                 start=(n == 0), stop=last)
-            if last:
-                mm.then_inc(sem["mm%d" % h], 1)
+            g.tensor.wait_ge(sem["arr%d_%d" % (k, c)], cnt)
+            mm(c, i, T["land%d" % k], False, n == len(away) - 1)
 
-    queues = [g.sync, g.scalar]
-    for h in range(NH):
-        g.vector.wait_ge(sem["mm%d" % h], 1)
-        g.vector.tensor_copy(T.ys[:, HW * h:HW * h + HW], T["acc%d" % h][:, 0:HW]).then_inc(sem["cp%d" % h], 1)
-        q = queues[h % 2]
-        q.wait_ge(sem["cp%d" % h], 1)
-        q.dma_start(T.y[:, HW * h:HW * h + HW], T.ys[:, HW * h:HW * h + HW]).then_inc(sem["st%d" % h], 16)
-    for h in range(NH):
-        queues[h % 2].wait_ge(sem["st%d" % h], 16)
-    g.wait_ge(sem.sent, sum(len(_bits(m)) for _, _, m in plan))
+    for c in range(NB):
+        g.vector.wait_ge(sem["mm%d" % c], 1)
+        g.vector.tensor_copy(cols(T.ys, c), T["acc%d" % c][:, 0:WID[c]]).then_inc(sem["cp%d" % c], 1)
+        q = queues[c % 2]
+        q.wait_ge(sem["cp%d" % c], 1)
+        q.dma_start(cols(T.y, c), cols(T.ys, c)).then_inc(sem["st%d" % c], 16)
+    for c in range(NB):
+        queues[c % 2].wait_ge(sem["st%d" % c], 16)
+    g.wait_ge(sem.sent, NB * sum(len(_bits(m)) for _, _, m in plan))

@@ -2,24 +2,28 @@ from concourse.bass import DstId, RemoteDMATransfer
 
 P, TK, DEG = 128, 512, 3
 NLAND = DEG - 1
-WID = [128, 256, 128]
-NB = len(WID)
-LO = [sum(WID[:c]) for c in range(NB)]
-ENG = 8
+BLK = [(0, 96), (96, 96), (192, 192), (384, 128)]
+ALT = 1
+NEAR = [1, 2, 3, 0]
+FARS = [0, 2, 3]
+LOADS = [(0, 192), (192, 192), (384, 128)]
+LD = [0, 0, 1, 2]
+NB = len(BLK)
 
 SCRATCH = {
     "xs": ("sbuf", [P, TK], "bfloat16"),
     "ws": ("sbuf", [P, DEG * P], "bfloat16"),
     "ys": ("sbuf", [P, TK], "bfloat16"),
+    "relay": ("sbuf", [P, BLK[ALT][1]], "bfloat16"),
 }
 for _k in range(NLAND):
     SCRATCH["land%d" % _k] = ("sbuf", [P, TK], "bfloat16")
-for _c in range(NB):
-    SCRATCH["acc%d" % _c] = ("psum", [P, 512], "float32")
+for _b in range(NB):
+    SCRATCH["acc%d" % _b] = ("psum", [P, 512], "float32")
 
-SEMAPHORES = ["sw", "sent"]
-for _c in range(NB):
-    SEMAPHORES += ["sx%d" % _c, "mm%d" % _c, "cp%d" % _c, "st%d" % _c] + ["arr%d_%d" % (k, _c) for k in range(NLAND)]
+SEMAPHORES = ["sw", "sent", "relay_%d" % ALT] + ["sx%d" % n for n in range(len(LOADS))]
+for _b in range(NB):
+    SEMAPHORES += ["mm%d" % _b, "cp%d" % _b, "st%d" % _b] + ["land%d_%d" % (k, _b) for k in range(NLAND)]
 
 
 def _bits(m):
@@ -31,26 +35,44 @@ def _slots(q, T):
     return [i for i in range(len(row)) if row[i] != q]
 
 
-def _plan(j, T, topo):
-    src = T.cores[j]
-    out = []
-    for q in range(len(T.cores)):
+def _away(a, b, topo):
+    return (topo.host(a), topo.chip(a)) != (topo.host(b), topo.chip(b))
+
+
+def _routes(T, topo):
+    M, C = T.tables["MASK"], T.cores
+    S = []
+    for q in range(len(C)):
         for k, i in enumerate(_slots(q, T)):
-            if T.tables["MASK"][q][i] == j:
-                out.append((T.cores[q], k))
-    out.sort(key=lambda e: len(_bits(topo.mask(src, e[0]))))
-    every = 0
-    for d, _ in out:
-        every |= topo.mask(src, d)
-    share = len(_bits(every)) // len(out)
-    taken, res = 0, []
-    for d, k in out:
-        block = [b for b in _bits(topo.mask(src, d)) if not (taken >> b) & 1][:share]
-        for b in block:
-            taken |= 1 << b
-        n = min(ENG, len(block))
-        res.append((d, k, sum(1 << b for b in block[::len(block) // n][:n])))
-    return res
+            j = M[q][i]
+            s, d, land = C[j], C[q], "land%d" % k
+            if not _away(s, d, topo):
+                S.append([s, d, "xs", land, NEAR, False])
+                continue
+            S.append([s, d, "xs", land, FARS, False])
+            co = [c for c in C if c != s and not _away(c, s, topo) and topo.die(c) != topo.die(s) and topo.may_write(c, d)]
+            got = [c for c in co if j in M[T.rank_of(c)]]
+            if got:
+                rc = T.rank_of(got[0])
+                S.append([got[0], d, "land%d" % _slots(rc, T).index(M[rc].index(j)), land, [ALT], True])
+            else:
+                S.append([s, co[0], "xs", "relay", [ALT], False])
+                S.append([co[0], d, "relay", land, [ALT], True])
+    E = []
+    for n, st in enumerate(S):
+        peers = [m for m in range(len(S)) if S[m][0] == st[0]]
+        offs = [m for m in peers if _away(st[0], S[m][1], topo)]
+        ons = [m for m in peers if m not in offs]
+        a, o = -1, 0
+        for m in offs:
+            a &= topo.mask(st[0], S[m][1])
+        for m in ons:
+            o |= topo.mask(st[0], S[m][1])
+        eoff = _bits(a) if offs else []
+        eon = [b for b in _bits(o) if b not in eoff]
+        grp, pool = (offs, eoff) if n in offs else (ons, eon)
+        E.append(sum(1 << b for b in pool[grp.index(n)::len(grp)]))
+    return S, E
 
 
 def rank_program(g, core, T, topo):
@@ -60,56 +82,77 @@ def rank_program(g, core, T, topo):
     row = T.tables["MASK"][rank]
     sem = T.sem
     queues = [g.sync, g.scalar]
+    S, E = _routes(T, topo)
+    mine = [n for n in range(len(S)) if S[n][0] == core]
 
-    def cols(t, c):
-        return t[:, LO[c]:LO[c] + WID[c]]
+    def view(name, b):
+        if name == "relay":
+            return T.relay[:]
+        return T[name][:, BLK[b][0]:BLK[b][0] + BLK[b][1]]
 
-    for c in range(NB):
-        queues[c % 2].dma_start(cols(T.xs, c), cols(T.x, c)).then_inc(sem["sx%d" % c], 16)
-    queues[NB % 2].dma_start(T.ws[:], T.w[:]).then_inc(sem.sw, 16)
+    def landed(name, b):
+        return [len(_bits(E[n])) for n in range(len(S)) if S[n][1] == core and S[n][3] == name and b in S[n][4]][0]
 
-    plan = _plan(rank, T, topo)
-    for c in range(NB):
-        g.wait_ge(sem["sx%d" % c], 16)
+    for n, (lo, w) in enumerate(LOADS):
+        queues[n % 2].dma_start(T.xs[:, lo:lo + w], T.x[:, lo:lo + w]).then_inc(sem["sx%d" % n], 16)
+    queues[len(LOADS) % 2].dma_start(T.ws[:], T.w[:]).then_inc(sem.sw, 16)
+
+    left, seen = 0, []
+    for step in range(len(NEAR)):
         transfers = []
-        for d, k, m in plan:
+        for n in mine:
+            _, d, sb, db, sched, is_pass = S[n]
+            if is_pass or step >= len(sched):
+                continue
+            b = sched[step]
+            if LD[b] not in seen:
+                g.wait_ge(sem["sx%d" % LD[b]], 16)
+                seen.append(LD[b])
             rid, pid = topo.addr(d, core)
-            transfers.append(RemoteDMATransfer(dst_ids=[DstId(rid=rid, pnc=pid)], dma_engine_mask=m,
-                                               remote_sem=sem["arr%d_%d" % (k, c)],
-                                               src=cols(T.xs, c), dst=cols(T["land%d" % k], c)))
+            transfers.append(RemoteDMATransfer(dst_ids=[DstId(rid=rid, pnc=pid)], dma_engine_mask=E[n],
+                                               remote_sem=sem["%s_%d" % (db, b)], src=view(sb, b), dst=view(db, b)))
+            left += len(_bits(E[n]))
         g.remote_dma_fused(transfers, local_sem=sem.sent)
+
+    for n in mine:
+        _, d, sb, db, sched, is_pass = S[n]
+        if is_pass:
+            rid, pid = topo.addr(d, core)
+            g.wait_ge(sem["%s_%d" % (sb, ALT)], landed(sb, ALT))
+            g.remote_dma(view(db, ALT), view(sb, ALT), sem["%s_%d" % (db, ALT)], sem.sent, pid, rid, E[n])
+            left += len(_bits(E[n]))
 
     def far(i):
         s = T.cores[row[i]]
-        return ((topo.host(s), topo.chip(s)) != (topo.host(core), topo.chip(core)), topo.die(s) != topo.die(core))
+        return (_away(s, core, topo), topo.die(s) != topo.die(core))
 
     slots = _slots(rank, T)
     own = [i for i in range(len(row)) if row[i] == rank]
     away = sorted(slots, key=far)
+    order = FARS + [ALT] if far(away[-1])[0] else NEAR
 
-    def mm(c, i, src, first, last):
-        ins = g.tensor.matmul(T["acc%d" % c][:, 0:WID[c]], T.ws[:, P * i:P * i + P], cols(src, c), start=first, stop=last)
+    def mm(b, i, name, first, last):
+        ins = g.tensor.matmul(T["acc%d" % b][:, 0:BLK[b][1]], T.ws[:, P * i:P * i + P], view(name, b), start=first, stop=last)
         if last:
-            ins.then_inc(sem["mm%d" % c], 1)
+            ins.then_inc(sem["mm%d" % b], 1)
 
     g.tensor.wait_ge(sem.sw, 16)
-    for c in range(NB):
-        g.tensor.wait_ge(sem["sx%d" % c], 16)
+    for b in range(NB):
+        g.tensor.wait_ge(sem["sx%d" % LD[b]], 16)
         for n, i in enumerate(own):
-            mm(c, i, T.xs, n == 0, False)
-    for c in range(NB):
+            mm(b, i, "xs", n == 0, False)
+    for b in order:
         for n, i in enumerate(away):
-            k = slots.index(i)
-            cnt = [len(_bits(m)) for d, kk, m in _plan(row[i], T, topo) if d == core and kk == k][0]
-            g.tensor.wait_ge(sem["arr%d_%d" % (k, c)], cnt)
-            mm(c, i, T["land%d" % k], False, n == len(away) - 1)
+            name = "land%d" % slots.index(i)
+            g.tensor.wait_ge(sem["%s_%d" % (name, b)], landed(name, b))
+            mm(b, i, name, False, n == len(away) - 1)
 
-    for c in range(NB):
-        g.vector.wait_ge(sem["mm%d" % c], 1)
-        g.vector.tensor_copy(cols(T.ys, c), T["acc%d" % c][:, 0:WID[c]]).then_inc(sem["cp%d" % c], 1)
-        q = queues[c % 2]
-        q.wait_ge(sem["cp%d" % c], 1)
-        q.dma_start(cols(T.y, c), cols(T.ys, c)).then_inc(sem["st%d" % c], 16)
-    for c in range(NB):
-        queues[c % 2].wait_ge(sem["st%d" % c], 16)
-    g.wait_ge(sem.sent, NB * sum(len(_bits(m)) for _, _, m in plan))
+    for n, b in enumerate(order):
+        g.vector.wait_ge(sem["mm%d" % b], 1)
+        g.vector.tensor_copy(view("ys", b), T["acc%d" % b][:, 0:BLK[b][1]]).then_inc(sem["cp%d" % b], 1)
+        q = queues[n % 2]
+        q.wait_ge(sem["cp%d" % b], 1)
+        q.dma_start(view("y", b), view("ys", b)).then_inc(sem["st%d" % b], 16)
+    for n, b in enumerate(order):
+        queues[n % 2].wait_ge(sem["st%d" % b], 16)
+    g.wait_ge(sem.sent, left)

@@ -2,11 +2,12 @@ from concourse.bass import DstId, RemoteDMATransfer
 
 P, TK, DEG = 128, 512, 3
 NLAND = DEG - 1
-BLK = [(0, 96), (96, 96), (192, 192), (384, 128)]
+BLK = [(0, 144), (144, 144), (288, 160), (448, 64)]
 ALT = 1
 NEAR = [1, 2, 3, 0]
+LATE = [None, 2, 3, 0, 1]
 FARS = [0, 2, 3]
-LOADS = [(0, 192), (192, 192), (384, 128)]
+LOADS = [(0, 288), (288, 160), (448, 64)]
 LD = [0, 0, 1, 2]
 NB = len(BLK)
 
@@ -58,19 +59,22 @@ def _routes(T, topo):
             else:
                 S.append([s, co[0], "xs", "relay", [ALT], False])
                 S.append([co[0], d, "relay", land, [ALT], True])
+    for st in S:
+        if st[4] is NEAR and [r for r in S if r[0] == st[0] and r[3] == "relay"]:
+            st[4] = LATE
     E = []
     for n, st in enumerate(S):
         peers = [m for m in range(len(S)) if S[m][0] == st[0]]
         offs = [m for m in peers if _away(st[0], S[m][1], topo)]
-        ons = [m for m in peers if m not in offs]
+        ons = [m for m in peers if m not in offs and S[m][3] != "relay"]
         a, o = -1, 0
         for m in offs:
             a &= topo.mask(st[0], S[m][1])
-        for m in ons:
+        for m in peers:
             o |= topo.mask(st[0], S[m][1])
         eoff = _bits(a) if offs else []
         eon = [b for b in _bits(o) if b not in eoff]
-        grp, pool = (offs, eoff) if n in offs else (ons, eon)
+        grp, pool = (offs, eoff) if n in offs else (ons, eon) if n in ons else ([n], eon)
         E.append(sum(1 << b for b in pool[grp.index(n)::len(grp)]))
     return S, E
 
@@ -98,11 +102,11 @@ def rank_program(g, core, T, topo):
     queues[len(LOADS) % 2].dma_start(T.ws[:], T.w[:]).then_inc(sem.sw, 16)
 
     left, seen = 0, []
-    for step in range(len(NEAR)):
+    for step in range(len(LATE)):
         transfers = []
         for n in mine:
             _, d, sb, db, sched, is_pass = S[n]
-            if is_pass or step >= len(sched):
+            if is_pass or step >= len(sched) or sched[step] is None:
                 continue
             b = sched[step]
             if LD[b] not in seen:
@@ -112,7 +116,8 @@ def rank_program(g, core, T, topo):
             transfers.append(RemoteDMATransfer(dst_ids=[DstId(rid=rid, pnc=pid)], dma_engine_mask=E[n],
                                                remote_sem=sem["%s_%d" % (db, b)], src=view(sb, b), dst=view(db, b)))
             left += len(_bits(E[n]))
-        g.remote_dma_fused(transfers, local_sem=sem.sent)
+        if transfers:
+            g.remote_dma_fused(transfers, local_sem=sem.sent)
 
     for n in mine:
         _, d, sb, db, sched, is_pass = S[n]
@@ -129,7 +134,10 @@ def rank_program(g, core, T, topo):
     slots = _slots(rank, T)
     own = [i for i in range(len(row)) if row[i] == rank]
     away = sorted(slots, key=far)
-    order = FARS + [ALT] if far(away[-1])[0] else NEAR
+    if far(away[-1])[0]:
+        order = FARS + [ALT]
+    else:
+        order = sorted(range(NB), key=lambda b: max(st[4].index(b) for st in S if st[1] == core and b in st[4]))
 
     def mm(b, i, name, first, last):
         ins = g.tensor.matmul(T["acc%d" % b][:, 0:BLK[b][1]], T.ws[:, P * i:P * i + P], view(name, b), start=first, stop=last)

@@ -2,27 +2,31 @@ from concourse.bass import DstId, RemoteDMATransfer
 
 P, TK, DEG = 128, 512, 3
 NLAND = DEG - 1
-BLK = [(0, 144), (144, 144), (288, 160), (448, 64)]
-ALT = 1
-NEAR = [1, 2, 3, 0]
-LATE = [None, 2, 3, 0, 1]
-FARS = [0, 2, 3]
-LOADS = [(0, 288), (288, 160), (448, 64)]
-LD = [0, 0, 1, 2]
+BLK = [(0, 80), (80, 80), (160, 80), (240, 80), (320, 128), (448, 64)]
+ALTS = [0, 2]
+FARS = [(1, 1), (3, 3), (4, 4), (5, 5)]
+NEAR = [(0, 0), (2, 2), (4, 4), (5, 5), (1, 1), (3, 3)]
+RELAY = [(0, 0), (2, 2)]
+LATE = [None, None, (4, 4), (5, 5), (0, 3)]
+PASS_AFTER = [2, 3]
+FAR_ORDER = [1, 3, 4, 0, 5, 2]
+LOADS = [(0, 160), (160, 160), (320, 192)]
+LD = [0, 0, 1, 1, 2, 2]
+NOFF = 4
 NB = len(BLK)
 
 SCRATCH = {
     "xs": ("sbuf", [P, TK], "bfloat16"),
     "ws": ("sbuf", [P, DEG * P], "bfloat16"),
     "ys": ("sbuf", [P, TK], "bfloat16"),
-    "relay": ("sbuf", [P, BLK[ALT][1]], "bfloat16"),
+    "relay": ("sbuf", [P, TK], "bfloat16"),
 }
 for _k in range(NLAND):
     SCRATCH["land%d" % _k] = ("sbuf", [P, TK], "bfloat16")
 for _b in range(NB):
     SCRATCH["acc%d" % _b] = ("psum", [P, 512], "float32")
 
-SEMAPHORES = ["sw", "sent", "relay_%d" % ALT] + ["sx%d" % n for n in range(len(LOADS))]
+SEMAPHORES = ["sw", "sent"] + ["relay_%d" % a for a in ALTS] + ["sx%d" % n for n in range(len(LOADS))]
 for _b in range(NB):
     SEMAPHORES += ["mm%d" % _b, "cp%d" % _b, "st%d" % _b] + ["land%d_%d" % (k, _b) for k in range(NLAND)]
 
@@ -42,6 +46,7 @@ def _away(a, b, topo):
 
 def _routes(T, topo):
     M, C = T.tables["MASK"], T.cores
+    PASS = [(a, a) for a in ALTS]
     S = []
     for q in range(len(C)):
         for k, i in enumerate(_slots(q, T)):
@@ -55,10 +60,10 @@ def _routes(T, topo):
             got = [c for c in co if j in M[T.rank_of(c)]]
             if got:
                 rc = T.rank_of(got[0])
-                S.append([got[0], d, "land%d" % _slots(rc, T).index(M[rc].index(j)), land, [ALT], True])
+                S.append([got[0], d, "land%d" % _slots(rc, T).index(M[rc].index(j)), land, PASS, True])
             else:
-                S.append([s, co[0], "xs", "relay", [ALT], False])
-                S.append([co[0], d, "relay", land, [ALT], True])
+                S.append([s, co[0], "xs", "relay", RELAY, False])
+                S.append([co[0], d, "relay", land, PASS, True])
     for st in S:
         if st[4] is NEAR and [r for r in S if r[0] == st[0] and r[3] == "relay"]:
             st[4] = LATE
@@ -75,7 +80,10 @@ def _routes(T, topo):
         eoff = _bits(a) if offs else []
         eon = [b for b in _bits(o) if b not in eoff]
         grp, pool = (offs, eoff) if n in offs else (ons, eon) if n in ons else ([n], eon)
-        E.append(sum(1 << b for b in pool[grp.index(n)::len(grp)]))
+        eng = pool[grp.index(n)::len(grp)]
+        if n in offs:
+            eng = eng[::max(1, len(eng) // NOFF)]
+        E.append(sum(1 << b for b in eng))
     return S, E
 
 
@@ -89,43 +97,51 @@ def rank_program(g, core, T, topo):
     S, E = _routes(T, topo)
     mine = [n for n in range(len(S)) if S[n][0] == core]
 
-    def view(name, b):
-        if name == "relay":
-            return T.relay[:]
-        return T[name][:, BLK[b][0]:BLK[b][0] + BLK[b][1]]
+    def view(name, b0, b1):
+        return T[name][:, BLK[b0][0]:BLK[b1][0] + BLK[b1][1]]
 
-    def landed(name, b):
-        return [len(_bits(E[n])) for n in range(len(S)) if S[n][1] == core and S[n][3] == name and b in S[n][4]][0]
+    def cover(name, b):
+        for n in range(len(S)):
+            if S[n][1] == core and S[n][3] == name:
+                for step, it in enumerate(S[n][4]):
+                    if it is not None and it[0] <= b <= it[1]:
+                        return sem["%s_%d" % (name, it[0])], len(_bits(E[n])), step
+        return None
 
     for n, (lo, w) in enumerate(LOADS):
-        queues[n % 2].dma_start(T.xs[:, lo:lo + w], T.x[:, lo:lo + w]).then_inc(sem["sx%d" % n], 16)
-    queues[len(LOADS) % 2].dma_start(T.ws[:], T.w[:]).then_inc(sem.sw, 16)
+        g.sync.dma_start(T.xs[:, lo:lo + w], T.x[:, lo:lo + w]).then_inc(sem["sx%d" % n], 16)
+    g.scalar.wait_ge(sem.sx0, 16)
+    g.scalar.dma_start(T.ws[:], T.w[:]).then_inc(sem.sw, 16)
 
-    left, seen = 0, []
-    for step in range(len(LATE)):
+    left, seen = [0], []
+    for step in range(len(NEAR)):
         transfers = []
         for n in mine:
             _, d, sb, db, sched, is_pass = S[n]
             if is_pass or step >= len(sched) or sched[step] is None:
                 continue
-            b = sched[step]
-            if LD[b] not in seen:
-                g.wait_ge(sem["sx%d" % LD[b]], 16)
-                seen.append(LD[b])
+            b0, b1 = sched[step]
+            for b in range(b0, b1 + 1):
+                if LD[b] not in seen:
+                    g.wait_ge(sem["sx%d" % LD[b]], 16)
+                    seen.append(LD[b])
             rid, pid = topo.addr(d, core)
             transfers.append(RemoteDMATransfer(dst_ids=[DstId(rid=rid, pnc=pid)], dma_engine_mask=E[n],
-                                               remote_sem=sem["%s_%d" % (db, b)], src=view(sb, b), dst=view(db, b)))
-            left += len(_bits(E[n]))
+                                               remote_sem=sem["%s_%d" % (db, b0)], src=view(sb, b0, b1), dst=view(db, b0, b1)))
+            left[0] += len(_bits(E[n]))
         if transfers:
             g.remote_dma_fused(transfers, local_sem=sem.sent)
-
-    for n in mine:
-        _, d, sb, db, sched, is_pass = S[n]
-        if is_pass:
-            rid, pid = topo.addr(d, core)
-            g.wait_ge(sem["%s_%d" % (sb, ALT)], landed(sb, ALT))
-            g.remote_dma(view(db, ALT), view(sb, ALT), sem["%s_%d" % (db, ALT)], sem.sent, pid, rid, E[n])
-            left += len(_bits(E[n]))
+        for k, a in enumerate(ALTS):
+            if PASS_AFTER[k] != step:
+                continue
+            for n in mine:
+                _, d, sb, db, sched, is_pass = S[n]
+                if is_pass:
+                    rid, pid = topo.addr(d, core)
+                    s_, c_, _ = cover(sb, a)
+                    g.wait_ge(s_, c_)
+                    g.remote_dma(view(db, a, a), view(sb, a, a), sem["%s_%d" % (db, a)], sem.sent, pid, rid, E[n])
+                    left[0] += len(_bits(E[n]))
 
     def far(i):
         s = T.cores[row[i]]
@@ -134,33 +150,42 @@ def rank_program(g, core, T, topo):
     slots = _slots(rank, T)
     own = [i for i in range(len(row)) if row[i] == rank]
     away = sorted(slots, key=far)
-    if far(away[-1])[0]:
-        order = FARS + [ALT]
-    else:
-        order = sorted(range(NB), key=lambda b: max(st[4].index(b) for st in S if st[1] == core and b in st[4]))
+    names = {i: "land%d" % slots.index(i) for i in slots}
 
     def mm(b, i, name, first, last):
-        ins = g.tensor.matmul(T["acc%d" % b][:, 0:BLK[b][1]], T.ws[:, P * i:P * i + P], view(name, b), start=first, stop=last)
+        ins = g.tensor.matmul(T["acc%d" % b][:, 0:BLK[b][1]], T.ws[:, P * i:P * i + P], view(name, b, b), start=first, stop=last)
         if last:
             ins.then_inc(sem["mm%d" % b], 1)
+
+    def arrive(b, i, last):
+        s_, c_, _ = cover(names[i], b)
+        g.tensor.wait_ge(s_, c_)
+        mm(b, i, names[i], False, last)
 
     g.tensor.wait_ge(sem.sw, 16)
     for b in range(NB):
         g.tensor.wait_ge(sem["sx%d" % LD[b]], 16)
         for n, i in enumerate(own):
             mm(b, i, "xs", n == 0, False)
-    for b in order:
-        for n, i in enumerate(away):
-            name = "land%d" % slots.index(i)
-            g.tensor.wait_ge(sem["%s_%d" % (name, b)], landed(name, b))
-            mm(b, i, name, False, n == len(away) - 1)
+    if far(away[-1])[0]:
+        order = FAR_ORDER
+        for i in away[:-1]:
+            for b in sorted(range(NB), key=lambda b: cover(names[i], b)[2]):
+                arrive(b, i, False)
+        for b in order:
+            arrive(b, away[-1], True)
+    else:
+        order = sorted(range(NB), key=lambda b: max(cover(names[i], b)[2] for i in away))
+        for b in order:
+            for n, i in enumerate(away):
+                arrive(b, i, n == len(away) - 1)
 
     for n, b in enumerate(order):
         g.vector.wait_ge(sem["mm%d" % b], 1)
-        g.vector.tensor_copy(view("ys", b), T["acc%d" % b][:, 0:BLK[b][1]]).then_inc(sem["cp%d" % b], 1)
+        g.vector.tensor_copy(view("ys", b, b), T["acc%d" % b][:, 0:BLK[b][1]]).then_inc(sem["cp%d" % b], 1)
         q = queues[n % 2]
         q.wait_ge(sem["cp%d" % b], 1)
-        q.dma_start(view("y", b), view("ys", b)).then_inc(sem["st%d" % b], 16)
+        q.dma_start(view("y", b, b), view("ys", b, b)).then_inc(sem["st%d" % b], 16)
     for n, b in enumerate(order):
         queues[n % 2].wait_ge(sem["st%d" % b], 16)
-    g.wait_ge(sem.sent, left)
+    g.wait_ge(sem.sent, left[0])

@@ -2,17 +2,17 @@ from concourse.bass import DstId, RemoteDMATransfer
 
 P, TK, DEG = 128, 512, 3
 NLAND = DEG - 1
-BLK = [(0, 80), (80, 80), (160, 80), (240, 80), (320, 128), (448, 64)]
-ALTS = [0, 2]
-FARS = [(1, 1), (3, 3), (4, 4), (5, 5)]
-NEAR = [(0, 0), (2, 2), (4, 4), (5, 5), (1, 1), (3, 3)]
-RELAY = [(0, 0), (2, 2)]
-LATE = [None, None, (4, 4), (5, 5), (0, 3)]
-PASS_AFTER = [2, 3]
-FAR_ORDER = [1, 3, 4, 0, 5, 2]
-LOADS = [(0, 160), (160, 160), (320, 192)]
-LD = [0, 0, 1, 1, 2, 2]
-NOFF = 4
+BLK = [(0, 80), (80, 104), (184, 80), (264, 80), (344, 104), (448, 64)]
+ALTS = [1, 3]
+FARS = [(0, 0, "A"), None, (2, 2, "A"), (4, 4, "A"), (5, 5, "A")]
+NEAR = [None, (1, 1, "CD"), (3, 3, "CD"), (4, 4, "CD"), None, (5, 5, "B"), [(0, 0, "C"), (2, 2, "D")]]
+RELAY = [None, (1, 1, "CD"), (3, 3, "CD")]
+LATE = [None, None, None, (4, 4, "CD"), (5, 5, "CD"), (0, 3, "CD")]
+WIDE = [[(0, 1, "A"), (2, 3, "D"), (4, 5, "D")], [(0, 1, "C"), (2, 3, "C"), (4, 5, "C")]]
+PASS_AFTER = 5
+FAR_ORDER = [0, 2, 4, 1, 5, 3]
+LOADS = [(0, 80), (80, 104), (184, 160), (344, 168)]
+LD = [0, 1, 2, 2, 3, 3]
 NB = len(BLK)
 
 SCRATCH = {
@@ -44,9 +44,15 @@ def _away(a, b, topo):
     return (topo.host(a), topo.chip(a)) != (topo.host(b), topo.chip(b))
 
 
+def _writes(sched, step, G):
+    it = sched[step] if step < len(sched) else None
+    if it is None:
+        return []
+    return [(b0, b1, G[k]) for b0, b1, k in (it if isinstance(it, list) else [it])]
+
+
 def _routes(T, topo):
     M, C = T.tables["MASK"], T.cores
-    PASS = [(a, a) for a in ALTS]
     S = []
     for q in range(len(C)):
         for k, i in enumerate(_slots(q, T)):
@@ -60,31 +66,34 @@ def _routes(T, topo):
             got = [c for c in co if j in M[T.rank_of(c)]]
             if got:
                 rc = T.rank_of(got[0])
-                S.append([got[0], d, "land%d" % _slots(rc, T).index(M[rc].index(j)), land, PASS, True])
+                S.append([got[0], d, "land%d" % _slots(rc, T).index(M[rc].index(j)), land, None, True])
             else:
                 S.append([s, co[0], "xs", "relay", RELAY, False])
-                S.append([co[0], d, "relay", land, PASS, True])
+                S.append([co[0], d, "relay", land, None, True])
+    wide = {}
     for st in S:
-        if st[4] is NEAR and [r for r in S if r[0] == st[0] and r[3] == "relay"]:
+        direct = [r for r in S if r[0] == st[0] and r[4] is FARS]
+        if st[5]:
+            st[4] = [(a, a, "B" if direct else "A") for a in ALTS]
+        elif st[4] is NEAR and [r for r in S if r[0] == st[0] and r[3] == "relay"]:
             st[4] = LATE
-    E = []
-    for n, st in enumerate(S):
-        peers = [m for m in range(len(S)) if S[m][0] == st[0]]
-        offs = [m for m in peers if _away(st[0], S[m][1], topo)]
-        ons = [m for m in peers if m not in offs and S[m][3] != "relay"]
-        a, o = -1, 0
-        for m in offs:
-            a &= topo.mask(st[0], S[m][1])
-        for m in peers:
-            o |= topo.mask(st[0], S[m][1])
-        eoff = _bits(a) if offs else []
-        eon = [b for b in _bits(o) if b not in eoff]
-        grp, pool = (offs, eoff) if n in offs else (ons, eon) if n in ons else ([n], eon)
-        eng = pool[grp.index(n)::len(grp)]
-        if n in offs:
-            eng = eng[::max(1, len(eng) // NOFF)]
-        E.append(sum(1 << b for b in eng))
-    return S, E
+        elif st[4] is NEAR and not direct:
+            wide[st[0]] = wide.get(st[0], -1) + 1
+            st[4] = WIDE[wide[st[0]]]
+    return S
+
+
+def _groups(c, S, topo):
+    a, o = -1, 0
+    for st in S:
+        if st[0] == c:
+            o |= topo.mask(c, st[1])
+            if _away(c, st[1], topo):
+                a &= topo.mask(c, st[1])
+    off = _bits(a)
+    on = [b for b in _bits(o) if b not in off]
+    L = {"A": off[0::2], "B": off[1::2], "C": on[0::2], "D": on[1::2], "CD": on}
+    return {k: sum(1 << b for b in v) for k, v in L.items()}
 
 
 def rank_program(g, core, T, topo):
@@ -94,18 +103,20 @@ def rank_program(g, core, T, topo):
     row = T.tables["MASK"][rank]
     sem = T.sem
     queues = [g.sync, g.scalar]
-    S, E = _routes(T, topo)
-    mine = [n for n in range(len(S)) if S[n][0] == core]
+    S = _routes(T, topo)
+    G = {c: _groups(c, S, topo) for c in T.cores}
+    mine = [st for st in S if st[0] == core]
 
     def view(name, b0, b1):
         return T[name][:, BLK[b0][0]:BLK[b1][0] + BLK[b1][1]]
 
     def cover(name, b):
-        for n in range(len(S)):
-            if S[n][1] == core and S[n][3] == name:
-                for step, it in enumerate(S[n][4]):
-                    if it is not None and it[0] <= b <= it[1]:
-                        return sem["%s_%d" % (name, it[0])], len(_bits(E[n])), step
+        for st in S:
+            if st[1] == core and st[3] == name:
+                for step in range(len(st[4])):
+                    for b0, b1, m in _writes(st[4], step, G[st[0]]):
+                        if b0 <= b <= b1:
+                            return sem["%s_%d" % (name, b0)], len(_bits(m)), step
         return None
 
     for n, (lo, w) in enumerate(LOADS):
@@ -114,34 +125,34 @@ def rank_program(g, core, T, topo):
     g.scalar.dma_start(T.ws[:], T.w[:]).then_inc(sem.sw, 16)
 
     left, seen = [0], []
-    for step in range(len(NEAR)):
+    steps = max(len(st[4]) for st in mine if not st[5])
+    for step in range(steps):
         transfers = []
-        for n in mine:
-            _, d, sb, db, sched, is_pass = S[n]
-            if is_pass or step >= len(sched) or sched[step] is None:
+        for _, d, sb, db, sched, is_pass in mine:
+            if is_pass:
                 continue
-            b0, b1 = sched[step]
-            for b in range(b0, b1 + 1):
-                if LD[b] not in seen:
-                    g.wait_ge(sem["sx%d" % LD[b]], 16)
-                    seen.append(LD[b])
-            rid, pid = topo.addr(d, core)
-            transfers.append(RemoteDMATransfer(dst_ids=[DstId(rid=rid, pnc=pid)], dma_engine_mask=E[n],
-                                               remote_sem=sem["%s_%d" % (db, b0)], src=view(sb, b0, b1), dst=view(db, b0, b1)))
-            left[0] += len(_bits(E[n]))
+            for b0, b1, m in _writes(sched, step, G[core]):
+                for b in range(b0, b1 + 1):
+                    if LD[b] not in seen:
+                        g.wait_ge(sem["sx%d" % LD[b]], 16)
+                        seen.append(LD[b])
+                rid, pid = topo.addr(d, core)
+                transfers.append(RemoteDMATransfer(dst_ids=[DstId(rid=rid, pnc=pid)], dma_engine_mask=m,
+                                                   remote_sem=sem["%s_%d" % (db, b0)], src=view(sb, b0, b1), dst=view(db, b0, b1)))
+                left[0] += len(_bits(m))
         if transfers:
             g.remote_dma_fused(transfers, local_sem=sem.sent)
-        for k, a in enumerate(ALTS):
-            if PASS_AFTER[k] != step:
-                continue
-            for n in mine:
-                _, d, sb, db, sched, is_pass = S[n]
-                if is_pass:
-                    rid, pid = topo.addr(d, core)
-                    s_, c_, _ = cover(sb, a)
-                    g.wait_ge(s_, c_)
-                    g.remote_dma(view(db, a, a), view(sb, a, a), sem["%s_%d" % (db, a)], sem.sent, pid, rid, E[n])
-                    left[0] += len(_bits(E[n]))
+        if step != min(PASS_AFTER, steps - 1):
+            continue
+        for _, d, sb, db, sched, is_pass in mine:
+            if is_pass:
+                for k in range(len(sched)):
+                    for a, _, m in _writes(sched, k, G[core]):
+                        rid, pid = topo.addr(d, core)
+                        s_, c_, _ = cover(sb, a)
+                        g.wait_ge(s_, c_)
+                        g.remote_dma(view(db, a, a), view(sb, a, a), sem["%s_%d" % (db, a)], sem.sent, pid, rid, m)
+                        left[0] += len(_bits(m))
 
     def far(i):
         s = T.cores[row[i]]

from concourse.bass import DstId, RemoteDMATransfer

P, TK, DEG = 128, 512, 3
NLAND = DEG - 1
BLK = [(0, 80), (80, 104), (184, 80), (264, 80), (344, 104), (448, 64)]
ALTS = [1, 3]
FARS = [(0, 0, "A"), None, (2, 2, "A"), (4, 4, "A"), (5, 5, "A")]
NEAR = [None, (1, 1, "CD"), (3, 3, "CD"), (4, 4, "CD"), None, (5, 5, "B"), [(0, 0, "C"), (2, 2, "D")]]
RELAY = [None, (1, 1, "CD"), (3, 3, "CD")]
LATE = [None, None, None, (4, 4, "CD"), (5, 5, "CD"), (0, 3, "CD")]
WIDE = [[(0, 1, "A"), (2, 3, "D"), (4, 5, "D")], [(0, 1, "C"), (2, 3, "C"), (4, 5, "C")]]
PASS_AFTER = 5
FAR_ORDER = [0, 2, 4, 1, 5, 3]
LOADS = [(0, 80), (80, 104), (184, 160), (344, 168)]
LD = [0, 1, 2, 2, 3, 3]
NB = len(BLK)

SCRATCH = {
    "xs": ("sbuf", [P, TK], "bfloat16"),
    "ws": ("sbuf", [P, DEG * P], "bfloat16"),
    "ys": ("sbuf", [P, TK], "bfloat16"),
    "relay": ("sbuf", [P, TK], "bfloat16"),
}
for _k in range(NLAND):
    SCRATCH["land%d" % _k] = ("sbuf", [P, TK], "bfloat16")
for _b in range(NB):
    SCRATCH["acc%d" % _b] = ("psum", [P, 512], "float32")

SEMAPHORES = ["sw", "sent"] + ["relay_%d" % a for a in ALTS] + ["sx%d" % n for n in range(len(LOADS))]
for _b in range(NB):
    SEMAPHORES += ["mm%d" % _b, "cp%d" % _b, "st%d" % _b] + ["land%d_%d" % (k, _b) for k in range(NLAND)]


def _bits(m):
    return [b for b in range(m.bit_length()) if (m >> b) & 1]


def _slots(q, T):
    row = T.tables["MASK"][q]
    return [i for i in range(len(row)) if row[i] != q]


def _away(a, b, topo):
    return (topo.host(a), topo.chip(a)) != (topo.host(b), topo.chip(b))


def _writes(sched, step, G):
    it = sched[step] if step < len(sched) else None
    if it is None:
        return []
    return [(b0, b1, G[k]) for b0, b1, k in (it if isinstance(it, list) else [it])]


def _routes(T, topo):
    M, C = T.tables["MASK"], T.cores
    S = []
    for q in range(len(C)):
        for k, i in enumerate(_slots(q, T)):
            j = M[q][i]
            s, d, land = C[j], C[q], "land%d" % k
            if not _away(s, d, topo):
                S.append([s, d, "xs", land, NEAR, False])
                continue
            S.append([s, d, "xs", land, FARS, False])
            co = [c for c in C if c != s and not _away(c, s, topo) and topo.die(c) != topo.die(s) and topo.may_write(c, d)]
            got = [c for c in co if j in M[T.rank_of(c)]]
            if got:
                rc = T.rank_of(got[0])
                S.append([got[0], d, "land%d" % _slots(rc, T).index(M[rc].index(j)), land, None, True])
            else:
                S.append([s, co[0], "xs", "relay", RELAY, False])
                S.append([co[0], d, "relay", land, None, True])
    wide = {}
    for st in S:
        direct = [r for r in S if r[0] == st[0] and r[4] is FARS]
        if st[5]:
            st[4] = [(a, a, "B" if direct else "A") for a in ALTS]
        elif st[4] is NEAR and [r for r in S if r[0] == st[0] and r[3] == "relay"]:
            st[4] = LATE
        elif st[4] is NEAR and not direct:
            wide[st[0]] = wide.get(st[0], -1) + 1
            st[4] = WIDE[wide[st[0]]]
    return S


def _groups(c, S, topo):
    a, o = -1, 0
    for st in S:
        if st[0] == c:
            o |= topo.mask(c, st[1])
            if _away(c, st[1], topo):
                a &= topo.mask(c, st[1])
    off = _bits(a)
    on = [b for b in _bits(o) if b not in off]
    L = {"A": off[0::2], "B": off[1::2], "C": on[0::2], "D": on[1::2], "CD": on}
    return {k: sum(1 << b for b in v) for k, v in L.items()}


def rank_program(g, core, T, topo):
    rank = T.rank_of(core)
    if rank is None:
        return
    row = T.tables["MASK"][rank]
    sem = T.sem
    queues = [g.sync, g.scalar]
    S = _routes(T, topo)
    G = {c: _groups(c, S, topo) for c in T.cores}
    mine = [st for st in S if st[0] == core]

    def view(name, b0, b1):
        return T[name][:, BLK[b0][0]:BLK[b1][0] + BLK[b1][1]]

    def cover(name, b):
        for st in S:
            if st[1] == core and st[3] == name:
                for step in range(len(st[4])):
                    for b0, b1, m in _writes(st[4], step, G[st[0]]):
                        if b0 <= b <= b1:
                            return sem["%s_%d" % (name, b0)], len(_bits(m)), step
        return None

    for n, (lo, w) in enumerate(LOADS):
        g.sync.dma_start(T.xs[:, lo:lo + w], T.x[:, lo:lo + w]).then_inc(sem["sx%d" % n], 16)
    g.scalar.wait_ge(sem.sx0, 16)
    g.scalar.dma_start(T.ws[:], T.w[:]).then_inc(sem.sw, 16)

    left, seen = [0], []
    steps = max(len(st[4]) for st in mine if not st[5])
    for step in range(steps):
        transfers = []
        for _, d, sb, db, sched, is_pass in mine:
            if is_pass:
                continue
            for b0, b1, m in _writes(sched, step, G[core]):
                for b in range(b0, b1 + 1):
                    if LD[b] not in seen:
                        g.wait_ge(sem["sx%d" % LD[b]], 16)
                        seen.append(LD[b])
                rid, pid = topo.addr(d, core)
                transfers.append(RemoteDMATransfer(dst_ids=[DstId(rid=rid, pnc=pid)], dma_engine_mask=m,
                                                   remote_sem=sem["%s_%d" % (db, b0)], src=view(sb, b0, b1), dst=view(db, b0, b1)))
                left[0] += len(_bits(m))
        if transfers:
            g.remote_dma_fused(transfers, local_sem=sem.sent)
        if step != min(PASS_AFTER, steps - 1):
            continue
        for _, d, sb, db, sched, is_pass in mine:
            if is_pass:
                for k in range(len(sched)):
                    for a, _, m in _writes(sched, k, G[core]):
                        rid, pid = topo.addr(d, core)
                        s_, c_, _ = cover(sb, a)
                        g.wait_ge(s_, c_)
                        g.remote_dma(view(db, a, a), view(sb, a, a), sem["%s_%d" % (db, a)], sem.sent, pid, rid, m)
                        left[0] += len(_bits(m))

    def far(i):
        s = T.cores[row[i]]
        return (_away(s, core, topo), topo.die(s) != topo.die(core))

    slots = _slots(rank, T)
    own = [i for i in range(len(row)) if row[i] == rank]
    away = sorted(slots, key=far)
    names = {i: "land%d" % slots.index(i) for i in slots}

    def mm(b, i, name, first, last):
        ins = g.tensor.matmul(T["acc%d" % b][:, 0:BLK[b][1]], T.ws[:, P * i:P * i + P], view(name, b, b), start=first, stop=last)
        if last:
            ins.then_inc(sem["mm%d" % b], 1)

    def arrive(b, i, last):
        s_, c_, _ = cover(names[i], b)
        g.tensor.wait_ge(s_, c_)
        mm(b, i, names[i], False, last)

    g.tensor.wait_ge(sem.sw, 16)
    for b in range(NB):
        g.tensor.wait_ge(sem["sx%d" % LD[b]], 16)
        for n, i in enumerate(own):
            mm(b, i, "xs", n == 0, False)
    if far(away[-1])[0]:
        order = FAR_ORDER
        for i in away[:-1]:
            for b in sorted(range(NB), key=lambda b: cover(names[i], b)[2]):
                arrive(b, i, False)
        for b in order:
            arrive(b, away[-1], True)
    else:
        order = sorted(range(NB), key=lambda b: max(cover(names[i], b)[2] for i in away))
        for b in order:
            for n, i in enumerate(away):
                arrive(b, i, n == len(away) - 1)

    for n, b in enumerate(order):
        g.vector.wait_ge(sem["mm%d" % b], 1)
        g.vector.tensor_copy(view("ys", b, b), T["acc%d" % b][:, 0:BLK[b][1]]).then_inc(sem["cp%d" % b], 1)
        q = queues[n % 2]
        q.wait_ge(sem["cp%d" % b], 1)
        q.dma_start(view("y", b, b), view("ys", b, b)).then_inc(sem["st%d" % b], 16)
    for n, b in enumerate(order):
        queues[n % 2].wait_ge(sem["st%d" % b], 16)
    g.wait_ge(sem.sent, left[0])
